import numpy as np
import ml_dtypes


def mxq(x, axis, fmt="e4m3"):
    dtype, down = {"e4m3": (ml_dtypes.float8_e4m3fn, 7), "e5m2": (ml_dtypes.float8_e5m2, 14)}[fmt]
    v = np.moveaxis(np.asarray(x, np.float32).astype(ml_dtypes.bfloat16).astype(np.float64), axis, -1)
    blocks = v.reshape(v.shape[:-1] + (-1, 32))
    amax = np.abs(blocks).max(-1, keepdims=True)
    byte = np.maximum(np.where(amax > 0, np.frexp(amax)[1] - 1 + 127, 0) - down, 1)
    scale = np.exp2(byte - 127.0)
    codes = (blocks / scale).astype(np.float32).astype(dtype).astype(np.float64)
    return np.moveaxis((codes * scale).reshape(v.shape), -1, axis)


WIDE = False


def mx_kscale(k):
    if not WIDE:
        return np.ones(k)
    levels = np.array([10, -10, 5, -5, 0])
    if k % 512:
        return np.exp2(np.random.permutation(np.resize(levels, k // 32))).repeat(32)
    a = np.empty((k // 512, 16))
    for p in range(k // 512):
        a[p, :8] = np.random.permutation(np.resize(levels, 8))
        for g in range(8):
            far = levels[np.abs(levels - a[p, g]) >= 10]
            a[p, g + 8] = far[np.random.randint(len(far))]
    return np.exp2(a.ravel()).repeat(32)


def f64(x):
    return np.asarray(x).astype(np.float64)


def striped(idx):
    return np.tile(idx.reshape(-1, 16).T, (8, 1)).astype(np.uint16)


def unstriped(offs):
    return offs[:16].T.reshape(-1).astype(np.int64)


def striped8(idx):
    return np.concatenate([x.reshape(-1, 16).T for x in idx]).astype(np.uint16)


def runs(offs, k):
    lists = np.stack([offs[16 * r : 16 * r + 16].T.reshape(-1) for r in range(8)]).astype(np.int64)
    return lists[np.arange(k) % 512 // 64]


def pack_weight(w):
    k, n = w.shape
    w = f64(np.asarray(w, np.float32).astype(ml_dtypes.bfloat16)).reshape(k // 32, 32, n)
    amax = np.abs(w).max(1)
    byte = np.clip(np.where(amax > 0, np.frexp(amax)[1] - 1 + 127 - 7, 1), 1, 254)
    scaled = (w * np.exp2(127.0 - byte)[:, None, :]).reshape(k, n).astype(np.float32)
    words = np.ascontiguousarray(scaled.reshape(k // 512, 128, 4, n).transpose(0, 1, 3, 2)).astype(ml_dtypes.float8_e4m3fn).view(np.uint8)
    return words, np.ascontiguousarray(byte.astype(np.uint8).reshape(k // 512, 16, n))


def unpack_weight(words, scales):
    g, p, n, _ = words.shape
    vals = np.ascontiguousarray(words).view(ml_dtypes.float8_e4m3fn).astype(np.float64) * np.repeat(np.exp2(scales.astype(np.float64) - 127.0), 8, axis=1)[..., None]
    return vals.transpose(0, 1, 3, 2).reshape(g * 512, n)

def planes(y):
    n, m = y.shape
    v = y.astype(np.float32).astype(ml_dtypes.bfloat16).astype(np.float64).reshape(n // 32, 32, m)
    top = np.abs(v).max(1)
    byte = np.clip(np.where(top > 0, np.frexp(top)[1] - 1 + 127 - 7, 1), 1, 254)
    codes = (v * np.exp2(127.0 - byte)[:, None, :]).reshape(n, m).astype(np.float32).astype(ml_dtypes.float8_e4m3fn).view(np.uint8)
    words = codes.reshape(n // 512, 128, 4, m).transpose(0, 1, 3, 2)
    return np.ascontiguousarray(words), np.ascontiguousarray(byte.astype(np.uint8).reshape(n // 512, 16, m))


K, T, S, H = 512, 2048, 512, 512


def setup_inputs():
    n = np.random.standard_normal
    s = mx_kscale(K)[:, None]
    u = mx_kscale(H)
    packed_xT = pack_weight(n((K, T)) * s)
    packed_w1 = pack_weight(n((K, H)) / np.sqrt(K) / s)
    packed_w2 = pack_weight(n((H, H)) / np.sqrt(H) / u[:, None])
    return {
        "x_words": packed_xT[0],
        "x_scales": packed_xT[1],
        "w1_words": packed_w1[0],
        "w1_scales": packed_w1[1],
        "gn": (np.random.uniform(0.5, 1.5, (H, 1)) * u[:, None]).astype(np.float32),
        "w2_words": packed_w2[0],
        "w2_scales": packed_w2[1],
        "offs": striped(np.random.permutation(T)[:S]),
        "n1": striped8(np.stack([np.random.permutation(S) for _ in range(8)])),
        "n2": striped8(np.stack([np.random.permutation(S) for _ in range(8)])),
        "n3": striped8(np.stack([np.random.permutation(S) for _ in range(8)])),
    }


def reference(x_words, x_scales, w1_words, w1_scales, gn, w2_words, w2_scales, offs, n1, n2, n3):
    xq = unpack_weight(x_words, x_scales)[:, unstriped(offs)]
    y = unpack_weight(w1_words, w1_scales).T @ xq
    ex = np.exp(0.5 * y)
    z = f64(gn) * ((2.0 * ex) / (ex + ex[np.arange(H)[:, None], runs(n1, H)] + ex[np.arange(H)[:, None], runs(n2, H)]))
    w2q = unpack_weight(w2_words, w2_scales)
    h = w2q.T @ mxq(z, 0, "e4m3")
    z2 = f64(gn) * (h / (np.abs(h[np.arange(H)[:, None], runs(n3, H)]) + 0.5))
    out_0 = (w2q.T @ mxq(z2, 0, "e4m3")) + 1.5 * y
    return (out_0,) + planes(out_0)

@@ -1,0 +1,261 @@
+from contextlib import ExitStack
+
+import concourse.mybir as mybir
+
+F32 = mybir.dt.float32
+BF16 = mybir.dt.bfloat16
+I32 = mybir.dt.int32
+U32 = mybir.dt.uint32
+U16 = mybir.dt.uint16
+U8 = mybir.dt.uint8
+FP8X4 = mybir.dt.float8_e4m3fn_x4
+ACT = mybir.ActivationFunctionType
+ALU = mybir.AluOpType
+
+P = 128
+PACK = 4
+T = 2048
+S = 512
+H = 512
+BANK = 512
+FLOPS = 3 * 2 * 512 * 512 * 512
+
+FIRST_CHUNKS = [(0, 256), (256, 256)]
+LAST_CHUNKS = [(0, 128), (128, 128), (256, 128), (384, 128)]
+
+
+def load_words(queue, tile, words):
+    queue.dma_start(out=tile[:].bitcast(I32), in_=words[0].rearrange("p n t -> p (n t)").bitcast(I32))
+
+
+def load_scales(queue, tile, scales):
+    rows = scales[0].bitcast(I32)
+    for q in range(4):
+        queue.dma_start(out=tile[32 * q : 32 * q + 4, :].bitcast(I32), in_=rows[4 * q : 4 * q + 4, :])
+
+
+def deal(nc, dealt, plain):
+    nc.vector.tensor_copy(
+        out=dealt[:].rearrange("p (t m) -> p m t", t=PACK),
+        in_=plain[:].rearrange("p (m t) -> p m t", t=PACK),
+    )
+
+
+def woven(tile):
+    return tile[:].rearrange("p (c i t) -> p c t i", i=4, t=PACK)
+
+
+def planar(ap):
+    return ap.rearrange("p t (c i) -> p c t i", i=4)
+
+
+def product(nc, psum, tag, w_words, w_scales, words, scales, width):
+    per_bank = BANK // width
+    banks = []
+    for b in range(PACK // per_bank):
+        bank = psum.tile([P, per_bank, width], F32, name=tag + str(b), tag=tag + str(b))
+        for u in range(per_bank):
+            cols = slice((b * per_bank + u) * P, (b * per_bank + u + 1) * P)
+            nc.tensor.matmul_mx(
+                out=bank[:, u, :],
+                lhsT=w_words[:, cols].bitcast(FP8X4),
+                lhsT_scale=w_scales[:, cols],
+                rhs=words.bitcast(FP8X4),
+                rhs_scale=scales,
+                start=True,
+                stop=True,
+            )
+        banks.append(bank)
+    return banks
+
+
+def tile_picked_itersharenorm_none_po_kernel(
+    tc, x_words, x_scales, w1_words, w1_scales, gn, w2_words, w2_scales, offs, n1, n2, n3, out_0, out_1, out_2
+):
+    nc = tc.nc
+    with ExitStack() as ctx:
+        keep = ctx.enter_context(tc.tile_pool(name="keep", bufs=1))
+        psum = ctx.enter_context(tc.psum_pool(name="psum", bufs=1))
+
+        def sb(name, shape, dtype):
+            return keep.tile(shape, dtype, name=name, align_bytes=64)
+
+        xw = sb("xw", [P, T], U32)
+        xs = sb("xs", [P, T], U8)
+        w1w = sb("w1w", [P, H], U32)
+        w1s = sb("w1s", [P, H], U8)
+        w2w = sb("w2w", [P, H], U32)
+        w2s = sb("w2s", [P, H], U8)
+        offs_sb = sb("offs_sb", [P, S // 16], U16)
+        n1_sb = sb("n1_sb", [P, S // 16], U16)
+        n2_sb = sb("n2_sb", [P, S // 16], U16)
+        n3_sb = sb("n3_sb", [P, S // 16], U16)
+        gain = sb("gain", [P, PACK], F32)
+
+        nc.vector.memset(xs[:].bitcast(I32), 0)
+        nc.vector.memset(w1s[:].bitcast(I32), 0)
+        nc.gpsimd.memset(w2s[:].bitcast(I32), 0)
+
+        load_words(nc.sync, xw, x_words)
+        nc.sync.dma_start(out=offs_sb[:], in_=offs)
+        load_scales(nc.scalar, xs, x_scales)
+        load_words(nc.sync, w1w, w1_words)
+        load_scales(nc.sync, w1s, w1_scales)
+        nc.sync.dma_start(out=n1_sb[:], in_=n1)
+        nc.sync.dma_start(out=n2_sb[:], in_=n2)
+        nc.sync.dma_start(out=n3_sb[:], in_=n3)
+        load_scales(nc.gpsimd, w2s, w2_scales)
+        load_words(nc.gpsimd, w2w, w2_words)
+        nc.gpsimd.dma_start(out=gain[:], in_=gn.rearrange("(p t) o -> p (t o)", t=PACK))
+
+        gs = sb("gs", [P, S], U8)
+        nc.vector.tensor_copy(out=gs[:], in_=xs[:].indirect(offs_sb[:]))
+        w1w_d = sb("w1w_d", [P, H], U32)
+        w1s_d = sb("w1s_d", [P, H], U8)
+        deal(nc, w1w_d, w1w)
+        deal(nc, w1s_d, w1s)
+
+        ex = [sb("ex%d" % t, [P, S], F32) for t in range(PACK)]
+        ex_own = sb("ex_own", [P, PACK, S], F32)
+        ex_gain = sb("ex_gain", [P, PACK, S], F32)
+        y_banks = []
+        for c, (c0, w) in enumerate(FIRST_CHUNKS):
+            gw = sb("gw%d" % c, [P, w], U32)
+            nc.vector.tensor_copy(out=gw[:], in_=xw[:].indirect(offs_sb[:, c0 // 16 : (c0 + w) // 16]))
+            y_banks.append(product(nc, psum, "y%d" % c, w1w_d, w1s_d, gw[:], gs[:, c0 : c0 + w], w))
+
+        w2w_d = sb("w2w_d", [P, H], U32)
+        w2s_d = sb("w2s_d", [P, H], U8)
+        deal(nc, w2w_d, w2w)
+        deal(nc, w2s_d, w2s)
+
+        half = FIRST_CHUNKS[0][1]
+        for t in range(PACK):
+            for c, (c0, w) in enumerate(FIRST_CHUNKS):
+                nc.scalar.activation(out=ex[t][:, c0 : c0 + w], in_=y_banks[c][t // 2][:, t % 2, :], func=ACT.Exp, scale=0.5)
+        for b in range(2):
+            nc.scalar.activation(out=ex_own[:, 2 * b : 2 * b + 2, half:], in_=y_banks[1][b][:], func=ACT.Exp, scale=0.5)
+
+        inv = [sb("inv%d" % t, [P, S], F32) for t in range(PACK)]
+        h_gain = sb("h_gain", [P, PACK, S], F32)
+        sums = []
+        for c, (c0, w) in enumerate(FIRST_CHUNKS):
+            part = sb("part%d" % c, [P, PACK, w], F32)
+            total = sb("total%d" % c, [P, PACK, w], F32)
+            lst = slice(c0 // 16, (c0 + w) // 16)
+            for t in range(PACK):
+                if c == 0:
+                    nc.vector.tensor_copy(out=ex_own[:, t, :half], in_=ex[t][:, :half])
+                if t > 0:
+                    nc.vector.tensor_tensor(total[:, t - 1, :], ex[t - 1][:].indirect(n2_sb[:, lst]), part[:, t - 1, :], ALU.add)
+                nc.vector.tensor_tensor(part[:, t, :], ex[t][:].indirect(n1_sb[:, lst]), ex_own[:, t, c0 : c0 + w], ALU.add)
+            nc.vector.tensor_tensor(total[:, 3, :], ex[3][:].indirect(n2_sb[:, lst]), part[:, 3, :], ALU.add)
+            sums.append(total)
+
+        h_banks = []
+        for c, (c0, w) in enumerate(FIRST_CHUNKS):
+            root = sb("root%d" % c, [P, PACK, w], F32)
+            recip = sb("recip%d" % c, [P, PACK, w], F32)
+            for t in range(PACK):
+                nc.scalar.activation(
+                    out=ex_gain[:, t, c0 : c0 + w], in_=ex[t][:, c0 : c0 + w], func=ACT.Copy, scale=gain[:, t : t + 1]
+                )
+            for b in range(2):
+                nc.scalar.activation(
+                    out=root[:, 2 * b : 2 * b + 2, :], in_=sums[c][:, 2 * b : 2 * b + 2, :], func=ACT.Abs_reciprocal_sqrt, scale=0.5
+                )
+                nc.scalar.activation(out=recip[:, 2 * b : 2 * b + 2, :], in_=root[:, 2 * b : 2 * b + 2, :], func=ACT.Square)
+            z = sb("z%d" % c, [P, PACK * w], BF16)
+            nc.vector.tensor_tensor(woven(z), planar(recip[:]), planar(ex_gain[:, :, c0 : c0 + w]), ALU.mult)
+            zw = sb("zw%d" % c, [P, w], U32)
+            zs = sb("zs%d" % c, [P, w], U8)
+            nc.vector.quantize_mx(out=zw[:].bitcast(FP8X4), scales=zs[:], in_=z[:])
+            h_banks.append(product(nc, psum, "h%d" % c, w2w_d, w2s_d, zw[:], zs[:], w))
+
+        for c, (c0, w) in enumerate(FIRST_CHUNKS):
+            banks = h_banks[c]
+            size = sb("size%d" % c, [P, PACK, w], F32)
+            root2 = sb("rootb%d" % c, [P, PACK, w], F32)
+            for b in range(2):
+                nc.scalar.activation(out=size[:, 2 * b : 2 * b + 2, :], in_=banks[b][:], func=ACT.Abs)
+                for u in range(2):
+                    t = 2 * b + u
+                    nc.vector.tensor_scalar(h_gain[:, t, c0 : c0 + w], banks[b][:, u, :], gain[:, t : t + 1], None, ALU.mult)
+                nc.scalar.activation(
+                    out=root2[:, 2 * b : 2 * b + 2, :], in_=size[:, 2 * b : 2 * b + 2, :], func=ACT.Abs_reciprocal_sqrt, bias=0.5
+                )
+                for u in range(2):
+                    t = 2 * b + u
+                    nc.scalar.activation(out=inv[t][:, c0 : c0 + w], in_=root2[:, t, :], func=ACT.Square)
+
+        y_part = sb("y_part", [P, PACK, S], F32)
+        for c, (c0, w) in enumerate(FIRST_CHUNKS):
+            for b in range(2):
+                nc.scalar.activation(
+                    out=y_part[:, 2 * b : 2 * b + 2, c0 : c0 + w], in_=y_banks[c][b][:], func=ACT.Copy, scale=1.5
+                )
+
+        z2f = [sb("z2f%d" % c, [P, PACK, w], F32) for c, (c0, w) in enumerate(FIRST_CHUNKS)]
+        for t, c in [(0, 0), (0, 1), (1, 0), (1, 1), (2, 0), (3, 0), (2, 1), (3, 1)]:
+            c0, w = FIRST_CHUNKS[c]
+            nc.vector.tensor_tensor(
+                z2f[c][:, t, :], inv[t][:].indirect(n3_sb[:, c0 // 16 : (c0 + w) // 16]), h_gain[:, t, c0 : c0 + w], ALU.mult
+            )
+
+        ow = sb("ow", [P, S], U32)
+        osc = sb("osc", [P, S], U8)
+        out_rows = out_0.rearrange("(p t) s -> p t s", t=PACK)
+        out_words = out_1[0].rearrange("p n t -> p (n t)").bitcast(I32)
+
+        def weave(on_vector, dst, src):
+            if on_vector:
+                nc.vector.tensor_copy(out=woven(dst), in_=planar(src))
+            else:
+                nc.scalar.copy(out=woven(dst), in_=planar(src))
+
+        def front(c):
+            c0, w = LAST_CHUNKS[c]
+            z2 = sb("z2_%d" % c, [P, PACK * w], BF16)
+            weave(c >= 2, z2, z2f[c // 2][:, :, c0 % half : c0 % half + w])
+            z2w = sb("z2w%d" % c, [P, w], U32)
+            z2s = sb("z2s%d" % c, [P, w], U8)
+            nc.vector.quantize_mx(out=z2w[:].bitcast(FP8X4), scales=z2s[:], in_=z2[:])
+            bank = psum.tile([P, PACK, w], F32, name="o%d" % c, tag="h%d%d" % (c // 2, c % 2))
+            for t in range(PACK):
+                cols = slice(t * P, (t + 1) * P)
+                nc.tensor.matmul_mx(
+                    out=bank[:, t, :],
+                    lhsT=w2w_d[:, cols].bitcast(FP8X4),
+                    lhsT_scale=w2s_d[:, cols],
+                    rhs=z2w[:].bitcast(FP8X4),
+                    rhs_scale=z2s[:],
+                    start=True,
+                    stop=True,
+                )
+            return bank
+
+        def middle(c, bank):
+            c0, w = LAST_CHUNKS[c]
+            res = sb("res%d" % c, [P, PACK, w], F32)
+            nc.vector.tensor_tensor(res[:], bank[:], y_part[:, :, c0 : c0 + w], ALU.add)
+            nc.sync.dma_start(out=out_rows[:, :, c0 : c0 + w], in_=res[:])
+            rb = sb("rb%d" % c, [P, PACK * w], BF16)
+            weave(c == 3, rb, res[:])
+            return rb
+
+        def back(c, rb):
+            c0, w = LAST_CHUNKS[c]
+            nc.vector.quantize_mx(out=ow[:, c0 : c0 + w].bitcast(FP8X4), scales=osc[:, c0 : c0 + w], in_=rb[:])
+            nc.sync.dma_start(out=out_words[:, c0 : c0 + w], in_=ow[:, c0 : c0 + w].bitcast(I32))
+
+        banks = [front(c) for c in range(4)]
+        rounded = []
+        for c in range(4):
+            rounded.append(middle(c, banks[c]))
+            if c > 0:
+                back(c - 1, rounded[c - 1])
+        back(3, rounded[3])
+        scale_rows = out_2[0].bitcast(I32)
+        for q in range(4):
+            queue = nc.sync if q % 2 == 0 else nc.scalar
+            queue.dma_start(out=scale_rows[4 * q : 4 * q + 4, :], in_=osc[32 * q : 32 * q + 4, :].bitcast(I32))

@@ -28,9 +28,9 @@ def load_words(queue, tile, words):
     queue.dma_start(out=tile[:].bitcast(I32), in_=words[0].rearrange("p n t -> p (n t)").bitcast(I32))
 
 
-def load_scales(queue, tile, scales):
+def load_scales(queues, tile, scales):
     rows = scales[0].bitcast(I32)
-    for q in range(4):
+    for q, queue in enumerate(queues):
         queue.dma_start(out=tile[32 * q : 32 * q + 4, :].bitcast(I32), in_=rows[4 * q : 4 * q + 4, :])
 
 
@@ -75,12 +75,13 @@ def tile_picked_itersharenorm_none_po_kernel(
     nc = tc.nc
     with ExitStack() as ctx:
         keep = ctx.enter_context(tc.tile_pool(name="keep", bufs=1))
+        table = ctx.enter_context(tc.tile_pool(name="table", bufs=1))
         psum = ctx.enter_context(tc.psum_pool(name="psum", bufs=1))
 
         def sb(name, shape, dtype):
             return keep.tile(shape, dtype, name=name, align_bytes=64)
 
-        xw = sb("xw", [P, T], U32)
+        xw = table.tile([P, T], U32, name="xw", offset=0, align_bytes=64)
         xs = sb("xs", [P, T], U8)
         w1w = sb("w1w", [P, H], U32)
         w1s = sb("w1s", [P, H], U8)
@@ -94,17 +95,17 @@ def tile_picked_itersharenorm_none_po_kernel(
 
         nc.vector.memset(xs[:].bitcast(I32), 0)
         nc.vector.memset(w1s[:].bitcast(I32), 0)
-        nc.gpsimd.memset(w2s[:].bitcast(I32), 0)
+        nc.vector.memset(w2s[:].bitcast(I32), 0)
 
-        load_words(nc.sync, xw, x_words)
+        load_words(nc.gpsimd, w1w, w1_words)
         nc.sync.dma_start(out=offs_sb[:], in_=offs)
-        load_scales(nc.scalar, xs, x_scales)
-        load_words(nc.sync, w1w, w1_words)
-        load_scales(nc.sync, w1s, w1_scales)
         nc.sync.dma_start(out=n1_sb[:], in_=n1)
         nc.sync.dma_start(out=n2_sb[:], in_=n2)
         nc.sync.dma_start(out=n3_sb[:], in_=n3)
-        load_scales(nc.gpsimd, w2s, w2_scales)
+        load_scales([nc.scalar, nc.scalar, nc.scalar, nc.gpsimd], xs, x_scales)
+        load_words(nc.sync, xw, x_words)
+        load_scales([nc.sync] * 4, w1s, w1_scales)
+        load_scales([nc.sync] * 4, w2s, w2_scales)
         load_words(nc.gpsimd, w2w, w2_words)
         nc.gpsimd.dma_start(out=gain[:], in_=gn.rearrange("(p t) o -> p (t o)", t=PACK))
 
@@ -115,85 +116,151 @@ def tile_picked_itersharenorm_none_po_kernel(
         deal(nc, w1w_d, w1w)
         deal(nc, w1s_d, w1s)
 
+        half = FIRST_CHUNKS[0][1]
         ex = [sb("ex%d" % t, [P, S], F32) for t in range(PACK)]
-        ex_own = sb("ex_own", [P, PACK, S], F32)
+        ex_own = [sb("ex_own%d" % c, [P, PACK, half], F32) for c in range(2)]
         ex_gain = sb("ex_gain", [P, PACK, S], F32)
-        y_banks = []
+        gw = []
         for c, (c0, w) in enumerate(FIRST_CHUNKS):
-            gw = sb("gw%d" % c, [P, w], U32)
-            nc.vector.tensor_copy(out=gw[:], in_=xw[:].indirect(offs_sb[:, c0 // 16 : (c0 + w) // 16]))
-            y_banks.append(product(nc, psum, "y%d" % c, w1w_d, w1s_d, gw[:], gs[:, c0 : c0 + w], w))
+            picked = sb("gw%d" % c, [P, w], U32)
+            nc.vector.tensor_copy(out=picked[:], in_=xw[:].indirect(offs_sb[:, c0 // 16 : (c0 + w) // 16]))
+            gw.append(picked)
+        y_banks = []
+        for t in range(PACK):
+            bank = psum.tile([P, S], F32, name="y%d" % t)
+            cols = slice(t * P, (t + 1) * P)
+            for c, (c0, w) in enumerate(FIRST_CHUNKS):
+                nc.tensor.matmul_mx(
+                    out=bank[:, c0 : c0 + w],
+                    lhsT=w1w_d[:, cols].bitcast(FP8X4),
+                    lhsT_scale=w1s_d[:, cols],
+                    rhs=gw[c][:].bitcast(FP8X4),
+                    rhs_scale=gs[:, c0 : c0 + w],
+                    start=True,
+                    stop=True,
+                )
+            y_banks.append(bank)
 
-        w2w_d = sb("w2w_d", [P, H], U32)
-        w2s_d = sb("w2s_d", [P, H], U8)
+        w2w_d = table.tile([P, H], U32, name="w2w_d", offset=0, align_bytes=64)
+        w2s_d = table.tile([P, H], U8, name="w2s_d", offset=4 * H, align_bytes=64)
         deal(nc, w2w_d, w2w)
         deal(nc, w2s_d, w2s)
 
-        half = FIRST_CHUNKS[0][1]
         for t in range(PACK):
-            for c, (c0, w) in enumerate(FIRST_CHUNKS):
-                nc.scalar.activation(out=ex[t][:, c0 : c0 + w], in_=y_banks[c][t // 2][:, t % 2, :], func=ACT.Exp, scale=0.5)
-        for b in range(2):
-            nc.scalar.activation(out=ex_own[:, 2 * b : 2 * b + 2, half:], in_=y_banks[1][b][:], func=ACT.Exp, scale=0.5)
+            nc.scalar.activation(out=ex[t][:], in_=y_banks[t][:], func=ACT.Exp, scale=0.5)
+            nc.scalar.activation(out=ex_own[0][:, t, :], in_=y_banks[t][:, :half], func=ACT.Exp, scale=0.5)
+        for t in range(PACK):
+            nc.sync.dma_start(out=ex_own[1][:, t, :], in_=ex[t][:, half:])
 
+        part = [sb("part%d" % c, [P, PACK, half], F32) for c in range(2)]
+        total = [sb("total%d" % c, [P, PACK, half], F32) for c in range(2)]
+        root = [sb("root%d" % c, [P, PACK, half], F32) for c in range(2)]
+        recip = [sb("recip%d" % c, [P, PACK, half], F32) for c in range(2)]
         inv = [sb("inv%d" % t, [P, S], F32) for t in range(PACK)]
         h_gain = sb("h_gain", [P, PACK, S], F32)
-        sums = []
-        for c, (c0, w) in enumerate(FIRST_CHUNKS):
-            part = sb("part%d" % c, [P, PACK, w], F32)
-            total = sb("total%d" % c, [P, PACK, w], F32)
-            lst = slice(c0 // 16, (c0 + w) // 16)
+        z = [sb("z%d" % c, [P, PACK * half], BF16) for c in range(2)]
+
+        def add_first(c, t, dst):
+            lst = slice(c * half // 16, (c + 1) * half // 16)
+            nc.vector.tensor_tensor(dst, ex[t][:].indirect(n1_sb[:, lst]), ex_own[c][:, t, :], ALU.add)
+
+        def add_second(c, t, src):
+            lst = slice(c * half // 16, (c + 1) * half // 16)
+            nc.vector.tensor_tensor(total[c][:, t, :], ex[t][:].indirect(n2_sb[:, lst]), src, ALU.add)
+
+        def gain_ex(c):
+            cols = slice(c * half, (c + 1) * half)
             for t in range(PACK):
-                if c == 0:
-                    nc.vector.tensor_copy(out=ex_own[:, t, :half], in_=ex[t][:, :half])
-                if t > 0:
-                    nc.vector.tensor_tensor(total[:, t - 1, :], ex[t - 1][:].indirect(n2_sb[:, lst]), part[:, t - 1, :], ALU.add)
-                nc.vector.tensor_tensor(part[:, t, :], ex[t][:].indirect(n1_sb[:, lst]), ex_own[:, t, c0 : c0 + w], ALU.add)
-            nc.vector.tensor_tensor(total[:, 3, :], ex[3][:].indirect(n2_sb[:, lst]), part[:, 3, :], ALU.add)
-            sums.append(total)
+                nc.scalar.activation(out=ex_gain[:, t, cols], in_=ex[t][:, cols], func=ACT.Copy, scale=gain[:, t : t + 1])
 
-        h_banks = []
-        for c, (c0, w) in enumerate(FIRST_CHUNKS):
-            root = sb("root%d" % c, [P, PACK, w], F32)
-            recip = sb("recip%d" % c, [P, PACK, w], F32)
-            for t in range(PACK):
-                nc.scalar.activation(
-                    out=ex_gain[:, t, c0 : c0 + w], in_=ex[t][:, c0 : c0 + w], func=ACT.Copy, scale=gain[:, t : t + 1]
-                )
-            for b in range(2):
-                nc.scalar.activation(
-                    out=root[:, 2 * b : 2 * b + 2, :], in_=sums[c][:, 2 * b : 2 * b + 2, :], func=ACT.Abs_reciprocal_sqrt, scale=0.5
-                )
-                nc.scalar.activation(out=recip[:, 2 * b : 2 * b + 2, :], in_=root[:, 2 * b : 2 * b + 2, :], func=ACT.Square)
-            z = sb("z%d" % c, [P, PACK * w], BF16)
-            nc.vector.tensor_tensor(woven(z), planar(recip[:]), planar(ex_gain[:, :, c0 : c0 + w]), ALU.mult)
-            zw = sb("zw%d" % c, [P, w], U32)
-            zs = sb("zs%d" % c, [P, w], U8)
-            nc.vector.quantize_mx(out=zw[:].bitcast(FP8X4), scales=zs[:], in_=z[:])
-            h_banks.append(product(nc, psum, "h%d" % c, w2w_d, w2s_d, zw[:], zs[:], w))
+        def invert_sum(c, lo, hi):
+            nc.scalar.activation(out=root[c][:, lo:hi, :], in_=total[c][:, lo:hi, :], func=ACT.Abs_reciprocal_sqrt, scale=0.5)
+            nc.scalar.activation(out=recip[c][:, lo:hi, :], in_=root[c][:, lo:hi, :], func=ACT.Square)
 
-        for c, (c0, w) in enumerate(FIRST_CHUNKS):
-            banks = h_banks[c]
-            size = sb("size%d" % c, [P, PACK, w], F32)
-            root2 = sb("rootb%d" % c, [P, PACK, w], F32)
-            for b in range(2):
-                nc.scalar.activation(out=size[:, 2 * b : 2 * b + 2, :], in_=banks[b][:], func=ACT.Abs)
-                for u in range(2):
-                    t = 2 * b + u
-                    nc.vector.tensor_scalar(h_gain[:, t, c0 : c0 + w], banks[b][:, u, :], gain[:, t : t + 1], None, ALU.mult)
-                nc.scalar.activation(
-                    out=root2[:, 2 * b : 2 * b + 2, :], in_=size[:, 2 * b : 2 * b + 2, :], func=ACT.Abs_reciprocal_sqrt, bias=0.5
-                )
-                for u in range(2):
-                    t = 2 * b + u
-                    nc.scalar.activation(out=inv[t][:, c0 : c0 + w], in_=root2[:, t, :], func=ACT.Square)
+        def make_z(c):
+            cols = slice(c * half, (c + 1) * half)
+            nc.vector.tensor_tensor(woven(z[c]), planar(recip[c][:]), planar(ex_gain[:, :, cols]), ALU.mult)
 
-        y_part = sb("y_part", [P, PACK, S], F32)
-        for c, (c0, w) in enumerate(FIRST_CHUNKS):
-            for b in range(2):
-                nc.scalar.activation(
-                    out=y_part[:, 2 * b : 2 * b + 2, c0 : c0 + w], in_=y_banks[c][b][:], func=ACT.Copy, scale=1.5
-                )
+        def second_product(c):
+            zw = sb("zw%d" % c, [P, half], U32)
+            zs = sb("zs%d" % c, [P, half], U8)
+            nc.vector.quantize_mx(out=zw[:].bitcast(FP8X4), scales=zs[:], in_=z[c][:])
+            return product(nc, psum, "h%d" % c, w2w_d, w2s_d, zw[:], zs[:], half)
+
+        size = [[sb("size%d%d" % (c, b), [P, 2, half], F32) for b in range(2)] for c in range(2)]
+        root2 = [[sb("rootb%d%d" % (c, b), [P, 2, half], F32) for b in range(2)] for c in range(2)]
+
+        def take_size(c, b, bank):
+            nc.scalar.activation(out=size[c][b][:], in_=bank[:], func=ACT.Abs)
+
+        def root_size(c, b):
+            nc.scalar.activation(out=root2[c][b][:], in_=size[c][b][:], func=ACT.Abs_reciprocal_sqrt, bias=0.5)
+
+        def square_size(c, b):
+            cols = slice(c * half, (c + 1) * half)
+            for u in range(2):
+                nc.scalar.activation(out=inv[2 * b + u][:, cols], in_=root2[c][b][:, u, :], func=ACT.Square)
+
+        def square_size_vector(c, b):
+            cols = slice(c * half, (c + 1) * half)
+            for u in range(2):
+                nc.vector.tensor_tensor(inv[2 * b + u][:, cols], root2[c][b][:, u, :], root2[c][b][:, u, :], ALU.mult)
+
+        def gain_h_scalar(c, b, bank):
+            cols = slice(c * half, (c + 1) * half)
+            for u in range(2):
+                t = 2 * b + u
+                nc.scalar.activation(out=h_gain[:, t, cols], in_=bank[:, u, :], func=ACT.Copy, scale=gain[:, t : t + 1])
+
+        def gain_h(c, b, bank):
+            cols = slice(c * half, (c + 1) * half)
+            for u in range(2):
+                t = 2 * b + u
+                nc.vector.tensor_scalar(h_gain[:, t, cols], bank[:, u, :], gain[:, t : t + 1], None, ALU.mult)
+
+        for t in range(PACK):
+            add_first(0, t, part[0][:, t, :])
+            if t > 0:
+                add_second(0, t - 1, part[0][:, t - 1, :])
+        add_first(1, 0, part[1][:, 0, :])
+        add_second(0, 3, part[0][:, 3, :])
+        gain_ex(0)
+        invert_sum(0, 0, 2)
+        invert_sum(0, 2, 4)
+        add_first(1, 1, part[1][:, 1, :])
+        add_second(1, 0, part[1][:, 0, :])
+        add_second(1, 1, part[1][:, 1, :])
+        make_z(0)
+        add_first(1, 2, recip[0][:, 0, :])
+        h0 = second_product(0)
+        add_first(1, 3, recip[0][:, 1, :])
+        add_second(1, 2, recip[0][:, 0, :])
+        add_second(1, 3, recip[0][:, 1, :])
+        gain_ex(1)
+        invert_sum(1, 0, 2)
+        take_size(0, 0, h0[0])
+        invert_sum(1, 2, 3)
+        invert_sum(1, 3, 4)
+        gain_h(0, 0, h0[0])
+        make_z(1)
+        take_size(0, 1, h0[1])
+        root_size(0, 0)
+        root_size(0, 1)
+        h1 = second_product(1)
+        square_size_vector(0, 0)
+        gain_h(0, 1, h0[1])
+        square_size_vector(0, 1)
+        y_part = ex_gain
+        take_size(1, 0, h1[0])
+        gain_h(1, 0, h1[0])
+        root_size(1, 0)
+        square_size(1, 0)
+        take_size(1, 1, h1[1])
+        root_size(1, 1)
+        square_size(1, 1)
+        gain_h_scalar(1, 1, h1[1])
+        for t in range(PACK):
+            nc.scalar.activation(out=y_part[:, t, :], in_=y_banks[t][:], func=ACT.Copy, scale=1.5)
 
         z2f = [sb("z2f%d" % c, [P, PACK, w], F32) for c, (c0, w) in enumerate(FIRST_CHUNKS)]
         for t, c in [(0, 0), (0, 1), (1, 0), (1, 1), (2, 0), (3, 0), (2, 1), (3, 1)]:
@@ -216,7 +283,7 @@ def tile_picked_itersharenorm_none_po_kernel(
         def front(c):
             c0, w = LAST_CHUNKS[c]
             z2 = sb("z2_%d" % c, [P, PACK * w], BF16)
-            weave(c >= 2, z2, z2f[c // 2][:, :, c0 % half : c0 % half + w])
+            weave(False, z2, z2f[c // 2][:, :, c0 % half : c0 % half + w])
             z2w = sb("z2w%d" % c, [P, w], U32)
             z2s = sb("z2s%d" % c, [P, w], U8)
             nc.vector.quantize_mx(out=z2w[:].bitcast(FP8X4), scales=z2s[:], in_=z2[:])

@@ -31,13 +31,13 @@ def load_words(queue, tile, words):
 def load_scales(queues, tile, scales):
     rows = scales[0].bitcast(I32)
     for q, queue in enumerate(queues):
-        queue.dma_start(out=tile[32 * q : 32 * q + 4, :].bitcast(I32), in_=rows[4 * q : 4 * q + 4, :])
+        queue.dma_start(out=tile[32 * q : 32 * q + 4, : scales.shape[2]].bitcast(I32), in_=rows[4 * q : 4 * q + 4, :])
 
 
 def deal(nc, dealt, plain):
     nc.vector.tensor_copy(
         out=dealt[:].rearrange("p (t m) -> p m t", t=PACK),
-        in_=plain[:].rearrange("p (m t) -> p m t", t=PACK),
+        in_=plain[:, :H].rearrange("p (m t) -> p m t", t=PACK),
     )
 
 
@@ -75,38 +75,36 @@ def tile_picked_itersharenorm_none_po_kernel(
     nc = tc.nc
     with ExitStack() as ctx:
         keep = ctx.enter_context(tc.tile_pool(name="keep", bufs=1))
-        table = ctx.enter_context(tc.tile_pool(name="table", bufs=1))
+        stage = ctx.enter_context(tc.tile_pool(name="stage", bufs=1))
         psum = ctx.enter_context(tc.psum_pool(name="psum", bufs=1))
 
         def sb(name, shape, dtype):
             return keep.tile(shape, dtype, name=name, align_bytes=64)
 
-        xw = table.tile([P, T], U32, name="xw", offset=0, align_bytes=64)
-        xs = sb("xs", [P, T], U8)
-        w1w = sb("w1w", [P, H], U32)
-        w1s = sb("w1s", [P, H], U8)
-        w2w = sb("w2w", [P, H], U32)
-        w2s = sb("w2s", [P, H], U8)
+        def staged(name, shape, dtype, offset):
+            return stage.tile(shape, dtype, name=name, offset=offset, align_bytes=64)
+
+        xs = staged("xs", [P, T], U8, 0)
+        w1w = staged("w1w", [P, H], U32, 5 * H)
+        w1s = staged("w1s", [P, H], U8, 9 * H)
+        xw = staged("xw", [P, T], U32, 10 * H)
         offs_sb = sb("offs_sb", [P, S // 16], U16)
         n1_sb = sb("n1_sb", [P, S // 16], U16)
         n2_sb = sb("n2_sb", [P, S // 16], U16)
         n3_sb = sb("n3_sb", [P, S // 16], U16)
         gain = sb("gain", [P, PACK], F32)
 
-        nc.vector.memset(xs[:].bitcast(I32), 0)
-        nc.vector.memset(w1s[:].bitcast(I32), 0)
-        nc.vector.memset(w2s[:].bitcast(I32), 0)
+        nc.gpsimd.memset(xs[:].bitcast(I32), 0)
+        nc.vector.memset(w1s[:, :H].bitcast(I32), 0)
 
-        load_words(nc.gpsimd, w1w, w1_words)
+        load_words(nc.gpsimd, xw, x_words)
         nc.sync.dma_start(out=offs_sb[:], in_=offs)
         nc.sync.dma_start(out=n1_sb[:], in_=n1)
         nc.sync.dma_start(out=n2_sb[:], in_=n2)
         nc.sync.dma_start(out=n3_sb[:], in_=n3)
-        load_scales([nc.scalar, nc.scalar, nc.scalar, nc.gpsimd], xs, x_scales)
-        load_words(nc.sync, xw, x_words)
+        load_scales([nc.scalar] * 4, xs, x_scales)
+        load_words(nc.gpsimd, w1w, w1_words)
         load_scales([nc.sync] * 4, w1s, w1_scales)
-        load_scales([nc.sync] * 4, w2s, w2_scales)
-        load_words(nc.gpsimd, w2w, w2_words)
         nc.gpsimd.dma_start(out=gain[:], in_=gn.rearrange("(p t) o -> p (t o)", t=PACK))
 
         gs = sb("gs", [P, S], U8)
@@ -115,6 +113,11 @@ def tile_picked_itersharenorm_none_po_kernel(
         w1s_d = sb("w1s_d", [P, H], U8)
         deal(nc, w1w_d, w1w)
         deal(nc, w1s_d, w1s)
+        w2s = staged("w2s", [P, H], U8, 0)
+        w2w = staged("w2w", [P, H], U32, H)
+        nc.gpsimd.memset(w2s[:].bitcast(I32), 0)
+        load_words(nc.sync, w2w, w2_words)
+        load_scales([nc.sync] * 4, w2s, w2_scales)
 
         half = FIRST_CHUNKS[0][1]
         ex = [sb("ex%d" % t, [P, S], F32) for t in range(PACK)]
@@ -141,8 +144,8 @@ def tile_picked_itersharenorm_none_po_kernel(
                 )
             y_banks.append(bank)
 
-        w2w_d = table.tile([P, H], U32, name="w2w_d", offset=0, align_bytes=64)
-        w2s_d = table.tile([P, H], U8, name="w2s_d", offset=4 * H, align_bytes=64)
+        w2w_d = staged("w2w_d", [P, H], U32, 9 * H + H // 2)
+        w2s_d = staged("w2s_d", [P, H], U8, 8 * H + H // 2)
         deal(nc, w2w_d, w2w)
         deal(nc, w2s_d, w2s)
 
@@ -168,55 +171,62 @@ def tile_picked_itersharenorm_none_po_kernel(
             lst = slice(c * half // 16, (c + 1) * half // 16)
             nc.vector.tensor_tensor(total[c][:, t, :], ex[t][:].indirect(n2_sb[:, lst]), src, ALU.add)
 
-        def gain_ex(c):
-            cols = slice(c * half, (c + 1) * half)
-            for t in range(PACK):
-                nc.scalar.activation(out=ex_gain[:, t, cols], in_=ex[t][:, cols], func=ACT.Copy, scale=gain[:, t : t + 1])
+        y_part = ex_gain
+        size = [sb("size%d" % c, [P, PACK, half], F32) for c in range(2)]
+        root2 = [sb("rootb%d" % c, [P, PACK, half], F32) for c in range(2)]
 
-        def invert_sum(c, lo, hi):
+        def gain_ex(c, t):
+            cols = slice(c * half, (c + 1) * half)
+            nc.scalar.activation(out=ex_gain[:, t, cols], in_=ex[t][:, cols], func=ACT.Copy, scale=gain[:, t : t + 1])
+
+        def root_sum(c, lo, hi):
             nc.scalar.activation(out=root[c][:, lo:hi, :], in_=total[c][:, lo:hi, :], func=ACT.Abs_reciprocal_sqrt, scale=0.5)
+
+        def square_sum(c, lo, hi):
             nc.scalar.activation(out=recip[c][:, lo:hi, :], in_=root[c][:, lo:hi, :], func=ACT.Square)
 
         def make_z(c):
             cols = slice(c * half, (c + 1) * half)
             nc.vector.tensor_tensor(woven(z[c]), planar(recip[c][:]), planar(ex_gain[:, :, cols]), ALU.mult)
 
-        def second_product(c):
-            zw = sb("zw%d" % c, [P, half], U32)
-            zs = sb("zs%d" % c, [P, half], U8)
-            nc.vector.quantize_mx(out=zw[:].bitcast(FP8X4), scales=zs[:], in_=z[c][:])
-            return product(nc, psum, "h%d" % c, w2w_d, w2s_d, zw[:], zs[:], half)
+        zw = [sb("zw%d" % c, [P, half], U32) for c in range(2)]
+        zs = [sb("zs%d" % c, [P, half], U8) for c in range(2)]
 
-        size = [[sb("size%d%d" % (c, b), [P, 2, half], F32) for b in range(2)] for c in range(2)]
-        root2 = [[sb("rootb%d%d" % (c, b), [P, 2, half], F32) for b in range(2)] for c in range(2)]
+        def quantise_z(c):
+            nc.vector.quantize_mx(out=zw[c][:].bitcast(FP8X4), scales=zs[c][:], in_=z[c][:])
 
-        def take_size(c, b, bank):
-            nc.scalar.activation(out=size[c][b][:], in_=bank[:], func=ACT.Abs)
+        def second_product(c, t, dst):
+            cols = slice(t * P, (t + 1) * P)
+            nc.tensor.matmul_mx(
+                out=dst,
+                lhsT=w2w_d[:, cols].bitcast(FP8X4),
+                lhsT_scale=w2s_d[:, cols],
+                rhs=zw[c][:].bitcast(FP8X4),
+                rhs_scale=zs[c][:],
+                start=True,
+                stop=True,
+            )
 
-        def root_size(c, b):
-            nc.scalar.activation(out=root2[c][b][:], in_=size[c][b][:], func=ACT.Abs_reciprocal_sqrt, bias=0.5)
+        def take_size(c, lo, hi, src):
+            nc.scalar.activation(out=size[c][:, lo:hi, :], in_=src, func=ACT.Abs)
 
-        def square_size(c, b):
+        def root_size(c, lo, hi):
+            nc.scalar.activation(out=root2[c][:, lo:hi, :], in_=size[c][:, lo:hi, :], func=ACT.Abs_reciprocal_sqrt, bias=0.5)
+
+        def square_size(c, t):
             cols = slice(c * half, (c + 1) * half)
-            for u in range(2):
-                nc.scalar.activation(out=inv[2 * b + u][:, cols], in_=root2[c][b][:, u, :], func=ACT.Square)
+            nc.scalar.activation(out=inv[t][:, cols], in_=root2[c][:, t, :], func=ACT.Square)
 
-        def square_size_vector(c, b):
+        def gain_h_scalar(c, t, src):
             cols = slice(c * half, (c + 1) * half)
-            for u in range(2):
-                nc.vector.tensor_tensor(inv[2 * b + u][:, cols], root2[c][b][:, u, :], root2[c][b][:, u, :], ALU.mult)
+            nc.scalar.activation(out=h_gain[:, t, cols], in_=src, func=ACT.Copy, scale=gain[:, t : t + 1])
 
-        def gain_h_scalar(c, b, bank):
+        def gain_h(c, t, src):
             cols = slice(c * half, (c + 1) * half)
-            for u in range(2):
-                t = 2 * b + u
-                nc.scalar.activation(out=h_gain[:, t, cols], in_=bank[:, u, :], func=ACT.Copy, scale=gain[:, t : t + 1])
+            nc.vector.tensor_scalar(h_gain[:, t, cols], src, gain[:, t : t + 1], None, ALU.mult)
 
-        def gain_h(c, b, bank):
-            cols = slice(c * half, (c + 1) * half)
-            for u in range(2):
-                t = 2 * b + u
-                nc.vector.tensor_scalar(h_gain[:, t, cols], bank[:, u, :], gain[:, t : t + 1], None, ALU.mult)
+        def keep_y_scalar(t):
+            nc.scalar.activation(out=y_part[:, t, :half], in_=y_banks[t][:, :half], func=ACT.Copy, scale=1.5)
 
         for t in range(PACK):
             add_first(0, t, part[0][:, t, :])
@@ -224,46 +234,67 @@ def tile_picked_itersharenorm_none_po_kernel(
                 add_second(0, t - 1, part[0][:, t - 1, :])
         add_first(1, 0, part[1][:, 0, :])
         add_second(0, 3, part[0][:, 3, :])
-        gain_ex(0)
-        invert_sum(0, 0, 2)
-        invert_sum(0, 2, 4)
+        for t in range(PACK):
+            gain_ex(0, t)
+        root_sum(0, 0, 2)
+        gain_ex(1, 0)
+        root_sum(0, 2, 4)
+        square_sum(0, 0, 2)
+        square_sum(0, 2, 4)
         add_first(1, 1, part[1][:, 1, :])
         add_second(1, 0, part[1][:, 0, :])
         add_second(1, 1, part[1][:, 1, :])
         make_z(0)
         add_first(1, 2, recip[0][:, 0, :])
-        h0 = second_product(0)
+        quantise_z(0)
+        h0 = [psum.tile([P, 2, half], F32, name="h0%d" % b, tag="h0%d" % b) for b in range(2)]
+        for t in range(PACK):
+            second_product(0, t, h0[t // 2][:, t % 2, :])
         add_first(1, 3, recip[0][:, 1, :])
         add_second(1, 2, recip[0][:, 0, :])
         add_second(1, 3, recip[0][:, 1, :])
-        gain_ex(1)
-        invert_sum(1, 0, 2)
-        take_size(0, 0, h0[0])
-        invert_sum(1, 2, 3)
-        invert_sum(1, 3, 4)
-        gain_h(0, 0, h0[0])
-        make_z(1)
-        take_size(0, 1, h0[1])
-        root_size(0, 0)
-        root_size(0, 1)
-        h1 = second_product(1)
-        square_size_vector(0, 0)
-        gain_h(0, 1, h0[1])
-        square_size_vector(0, 1)
-        y_part = ex_gain
-        take_size(1, 0, h1[0])
-        gain_h(1, 0, h1[0])
-        root_size(1, 0)
-        square_size(1, 0)
-        take_size(1, 1, h1[1])
-        root_size(1, 1)
-        square_size(1, 1)
-        gain_h_scalar(1, 1, h1[1])
+        for t in range(1, PACK):
+            gain_ex(1, t)
+        root_sum(1, 0, 2)
+        keep_y_scalar(0)
+        keep_y_scalar(1)
+        square_sum(1, 0, 2)
+        take_size(0, 0, 2, h0[0][:])
+        take_size(0, 2, 4, h0[1][:])
+        root_sum(1, 2, 3)
+        root_sum(1, 3, 4)
+        square_sum(1, 2, 3)
+        square_sum(1, 3, 4)
         for t in range(PACK):
-            nc.scalar.activation(out=y_part[:, t, :], in_=y_banks[t][:], func=ACT.Copy, scale=1.5)
+            gain_h(0, t, h0[t // 2][:, t % 2, :])
+        make_z(1)
+        root_size(0, 0, 2)
+        root_size(0, 2, 4)
+        for t in range(PACK):
+            square_size(0, t)
+        quantise_z(1)
+        for t in range(PACK):
+            nc.vector.tensor_scalar(y_part[:, t, half:], y_banks[t][:, half:], 1.5, None, ALU.mult)
+        h1 = [psum.tile([P, 2, half], F32, name="h1%d" % b, tag="h1%d" % b) for b in range(2)]
+        for u in range(2):
+            for b in range(2):
+                second_product(1, 2 * u + b, h1[b][:, u, :])
+            for b in range(2):
+                take_size(1, 2 * u + b, 2 * u + b + 1, h1[b][:, u : u + 1, :])
+            if u == 0:
+                for b in range(2):
+                    gain_h(1, b, h1[b][:, 0, :])
+            for b in range(2):
+                root_size(1, 2 * u + b, 2 * u + b + 1)
+            for b in range(2):
+                square_size(1, 2 * u + b)
+        for b in range(2):
+            gain_h_scalar(1, 2 + b, h1[b][:, 1, :])
+        keep_y_scalar(2)
+        keep_y_scalar(3)
 
         z2f = [sb("z2f%d" % c, [P, PACK, w], F32) for c, (c0, w) in enumerate(FIRST_CHUNKS)]
-        for t, c in [(0, 0), (0, 1), (1, 0), (1, 1), (2, 0), (3, 0), (2, 1), (3, 1)]:
+        for t, c in [(0, 0), (1, 0), (0, 1), (2, 0), (3, 0), (1, 1), (2, 1), (3, 1)]:
             c0, w = FIRST_CHUNKS[c]
             nc.vector.tensor_tensor(
                 z2f[c][:, t, :], inv[t][:].indirect(n3_sb[:, c0 // 16 : (c0 + w) // 16]), h_gain[:, t, c0 : c0 + w], ALU.mult

from contextlib import ExitStack

import concourse.mybir as mybir

F32 = mybir.dt.float32
BF16 = mybir.dt.bfloat16
I32 = mybir.dt.int32
U32 = mybir.dt.uint32
U16 = mybir.dt.uint16
U8 = mybir.dt.uint8
FP8X4 = mybir.dt.float8_e4m3fn_x4
ACT = mybir.ActivationFunctionType
ALU = mybir.AluOpType

P = 128
PACK = 4
T = 2048
S = 512
H = 512
BANK = 512
FLOPS = 3 * 2 * 512 * 512 * 512

FIRST_CHUNKS = [(0, 256), (256, 256)]
LAST_CHUNKS = [(0, 128), (128, 128), (256, 128), (384, 128)]


def load_words(queue, tile, words):
    queue.dma_start(out=tile[:].bitcast(I32), in_=words[0].rearrange("p n t -> p (n t)").bitcast(I32))


def load_scales(queues, tile, scales):
    rows = scales[0].bitcast(I32)
    for q, queue in enumerate(queues):
        queue.dma_start(out=tile[32 * q : 32 * q + 4, : scales.shape[2]].bitcast(I32), in_=rows[4 * q : 4 * q + 4, :])


def deal(nc, dealt, plain):
    nc.vector.tensor_copy(
        out=dealt[:].rearrange("p (t m) -> p m t", t=PACK),
        in_=plain[:, :H].rearrange("p (m t) -> p m t", t=PACK),
    )


def woven(tile):
    return tile[:].rearrange("p (c i t) -> p c t i", i=4, t=PACK)


def planar(ap):
    return ap.rearrange("p t (c i) -> p c t i", i=4)


def product(nc, psum, tag, w_words, w_scales, words, scales, width):
    per_bank = BANK // width
    banks = []
    for b in range(PACK // per_bank):
        bank = psum.tile([P, per_bank, width], F32, name=tag + str(b), tag=tag + str(b))
        for u in range(per_bank):
            cols = slice((b * per_bank + u) * P, (b * per_bank + u + 1) * P)
            nc.tensor.matmul_mx(
                out=bank[:, u, :],
                lhsT=w_words[:, cols].bitcast(FP8X4),
                lhsT_scale=w_scales[:, cols],
                rhs=words.bitcast(FP8X4),
                rhs_scale=scales,
                start=True,
                stop=True,
            )
        banks.append(bank)
    return banks


def tile_picked_itersharenorm_none_po_kernel(
    tc, x_words, x_scales, w1_words, w1_scales, gn, w2_words, w2_scales, offs, n1, n2, n3, out_0, out_1, out_2
):
    nc = tc.nc
    with ExitStack() as ctx:
        keep = ctx.enter_context(tc.tile_pool(name="keep", bufs=1))
        stage = ctx.enter_context(tc.tile_pool(name="stage", bufs=1))
        psum = ctx.enter_context(tc.psum_pool(name="psum", bufs=1))

        def sb(name, shape, dtype):
            return keep.tile(shape, dtype, name=name, align_bytes=64)

        def staged(name, shape, dtype, offset):
            return stage.tile(shape, dtype, name=name, offset=offset, align_bytes=64)

        xs = staged("xs", [P, T], U8, 0)
        w1w = staged("w1w", [P, H], U32, 5 * H)
        w1s = staged("w1s", [P, H], U8, 9 * H)
        xw = staged("xw", [P, T], U32, 10 * H)
        offs_sb = sb("offs_sb", [P, S // 16], U16)
        n1_sb = sb("n1_sb", [P, S // 16], U16)
        n2_sb = sb("n2_sb", [P, S // 16], U16)
        n3_sb = sb("n3_sb", [P, S // 16], U16)
        gain = sb("gain", [P, PACK], F32)

        nc.gpsimd.memset(xs[:].bitcast(I32), 0)
        nc.vector.memset(w1s[:, :H].bitcast(I32), 0)

        load_words(nc.gpsimd, xw, x_words)
        nc.sync.dma_start(out=offs_sb[:], in_=offs)
        nc.sync.dma_start(out=n1_sb[:], in_=n1)
        nc.sync.dma_start(out=n2_sb[:], in_=n2)
        nc.sync.dma_start(out=n3_sb[:], in_=n3)
        load_scales([nc.scalar] * 4, xs, x_scales)
        load_words(nc.gpsimd, w1w, w1_words)
        load_scales([nc.sync] * 4, w1s, w1_scales)
        nc.gpsimd.dma_start(out=gain[:], in_=gn.rearrange("(p t) o -> p (t o)", t=PACK))

        gs = sb("gs", [P, S], U8)
        nc.vector.tensor_copy(out=gs[:], in_=xs[:].indirect(offs_sb[:]))
        w1w_d = sb("w1w_d", [P, H], U32)
        w1s_d = sb("w1s_d", [P, H], U8)
        deal(nc, w1w_d, w1w)
        deal(nc, w1s_d, w1s)
        w2s = staged("w2s", [P, H], U8, 0)
        w2w = staged("w2w", [P, H], U32, H)
        nc.gpsimd.memset(w2s[:].bitcast(I32), 0)
        load_words(nc.sync, w2w, w2_words)
        load_scales([nc.sync] * 4, w2s, w2_scales)

        half = FIRST_CHUNKS[0][1]
        ex = [sb("ex%d" % t, [P, S], F32) for t in range(PACK)]
        ex_own = [sb("ex_own%d" % c, [P, PACK, half], F32) for c in range(2)]
        ex_gain = sb("ex_gain", [P, PACK, S], F32)
        gw = []
        for c, (c0, w) in enumerate(FIRST_CHUNKS):
            picked = sb("gw%d" % c, [P, w], U32)
            nc.vector.tensor_copy(out=picked[:], in_=xw[:].indirect(offs_sb[:, c0 // 16 : (c0 + w) // 16]))
            gw.append(picked)
        y_banks = []
        for t in range(PACK):
            bank = psum.tile([P, S], F32, name="y%d" % t)
            cols = slice(t * P, (t + 1) * P)
            for c, (c0, w) in enumerate(FIRST_CHUNKS):
                nc.tensor.matmul_mx(
                    out=bank[:, c0 : c0 + w],
                    lhsT=w1w_d[:, cols].bitcast(FP8X4),
                    lhsT_scale=w1s_d[:, cols],
                    rhs=gw[c][:].bitcast(FP8X4),
                    rhs_scale=gs[:, c0 : c0 + w],
                    start=True,
                    stop=True,
                )
            y_banks.append(bank)

        w2w_d = staged("w2w_d", [P, H], U32, 9 * H + H // 2)
        w2s_d = staged("w2s_d", [P, H], U8, 8 * H + H // 2)
        deal(nc, w2w_d, w2w)
        deal(nc, w2s_d, w2s)

        for t in range(PACK):
            nc.scalar.activation(out=ex[t][:], in_=y_banks[t][:], func=ACT.Exp, scale=0.5)
            nc.scalar.activation(out=ex_own[0][:, t, :], in_=y_banks[t][:, :half], func=ACT.Exp, scale=0.5)
        for t in range(PACK):
            nc.sync.dma_start(out=ex_own[1][:, t, :], in_=ex[t][:, half:])

        part = [sb("part%d" % c, [P, PACK, half], F32) for c in range(2)]
        total = [sb("total%d" % c, [P, PACK, half], F32) for c in range(2)]
        root = [sb("root%d" % c, [P, PACK, half], F32) for c in range(2)]
        recip = [sb("recip%d" % c, [P, PACK, half], F32) for c in range(2)]
        inv = [sb("inv%d" % t, [P, S], F32) for t in range(PACK)]
        h_gain = sb("h_gain", [P, PACK, S], F32)
        z = [sb("z%d" % c, [P, PACK * half], BF16) for c in range(2)]

        def add_first(c, t, dst):
            lst = slice(c * half // 16, (c + 1) * half // 16)
            nc.vector.tensor_tensor(dst, ex[t][:].indirect(n1_sb[:, lst]), ex_own[c][:, t, :], ALU.add)

        def add_second(c, t, src):
            lst = slice(c * half // 16, (c + 1) * half // 16)
            nc.vector.tensor_tensor(total[c][:, t, :], ex[t][:].indirect(n2_sb[:, lst]), src, ALU.add)

        y_part = ex_gain
        size = [sb("size%d" % c, [P, PACK, half], F32) for c in range(2)]
        root2 = [sb("rootb%d" % c, [P, PACK, half], F32) for c in range(2)]

        def gain_ex(c, t):
            cols = slice(c * half, (c + 1) * half)
            nc.scalar.activation(out=ex_gain[:, t, cols], in_=ex[t][:, cols], func=ACT.Copy, scale=gain[:, t : t + 1])

        def root_sum(c, lo, hi):
            nc.scalar.activation(out=root[c][:, lo:hi, :], in_=total[c][:, lo:hi, :], func=ACT.Abs_reciprocal_sqrt, scale=0.5)

        def square_sum(c, lo, hi):
            nc.scalar.activation(out=recip[c][:, lo:hi, :], in_=root[c][:, lo:hi, :], func=ACT.Square)

        def make_z(c):
            cols = slice(c * half, (c + 1) * half)
            nc.vector.tensor_tensor(woven(z[c]), planar(recip[c][:]), planar(ex_gain[:, :, cols]), ALU.mult)

        zw = [sb("zw%d" % c, [P, half], U32) for c in range(2)]
        zs = [sb("zs%d" % c, [P, half], U8) for c in range(2)]

        def quantise_z(c):
            nc.vector.quantize_mx(out=zw[c][:].bitcast(FP8X4), scales=zs[c][:], in_=z[c][:])

        def second_product(c, t, dst):
            cols = slice(t * P, (t + 1) * P)
            nc.tensor.matmul_mx(
                out=dst,
                lhsT=w2w_d[:, cols].bitcast(FP8X4),
                lhsT_scale=w2s_d[:, cols],
                rhs=zw[c][:].bitcast(FP8X4),
                rhs_scale=zs[c][:],
                start=True,
                stop=True,
            )

        def take_size(c, lo, hi, src):
            nc.scalar.activation(out=size[c][:, lo:hi, :], in_=src, func=ACT.Abs)

        def root_size(c, lo, hi):
            nc.scalar.activation(out=root2[c][:, lo:hi, :], in_=size[c][:, lo:hi, :], func=ACT.Abs_reciprocal_sqrt, bias=0.5)

        def square_size(c, t):
            cols = slice(c * half, (c + 1) * half)
            nc.scalar.activation(out=inv[t][:, cols], in_=root2[c][:, t, :], func=ACT.Square)

        def gain_h_scalar(c, t, src):
            cols = slice(c * half, (c + 1) * half)
            nc.scalar.activation(out=h_gain[:, t, cols], in_=src, func=ACT.Copy, scale=gain[:, t : t + 1])

        def gain_h(c, t, src):
            cols = slice(c * half, (c + 1) * half)
            nc.vector.tensor_scalar(h_gain[:, t, cols], src, gain[:, t : t + 1], None, ALU.mult)

        def keep_y_scalar(t):
            nc.scalar.activation(out=y_part[:, t, :half], in_=y_banks[t][:, :half], func=ACT.Copy, scale=1.5)

        for t in range(PACK):
            add_first(0, t, part[0][:, t, :])
            if t > 0:
                add_second(0, t - 1, part[0][:, t - 1, :])
        add_first(1, 0, part[1][:, 0, :])
        add_second(0, 3, part[0][:, 3, :])
        for t in range(PACK):
            gain_ex(0, t)
        root_sum(0, 0, 2)
        gain_ex(1, 0)
        root_sum(0, 2, 4)
        square_sum(0, 0, 2)
        square_sum(0, 2, 4)
        add_first(1, 1, part[1][:, 1, :])
        add_second(1, 0, part[1][:, 0, :])
        add_second(1, 1, part[1][:, 1, :])
        make_z(0)
        add_first(1, 2, recip[0][:, 0, :])
        quantise_z(0)
        h0 = [psum.tile([P, 2, half], F32, name="h0%d" % b, tag="h0%d" % b) for b in range(2)]
        for t in range(PACK):
            second_product(0, t, h0[t // 2][:, t % 2, :])
        add_first(1, 3, recip[0][:, 1, :])
        add_second(1, 2, recip[0][:, 0, :])
        add_second(1, 3, recip[0][:, 1, :])
        for t in range(1, PACK):
            gain_ex(1, t)
        root_sum(1, 0, 2)
        keep_y_scalar(0)
        keep_y_scalar(1)
        square_sum(1, 0, 2)
        take_size(0, 0, 2, h0[0][:])
        take_size(0, 2, 4, h0[1][:])
        root_sum(1, 2, 3)
        root_sum(1, 3, 4)
        square_sum(1, 2, 3)
        square_sum(1, 3, 4)
        for t in range(PACK):
            gain_h(0, t, h0[t // 2][:, t % 2, :])
        make_z(1)
        root_size(0, 0, 2)
        root_size(0, 2, 4)
        for t in range(PACK):
            square_size(0, t)
        quantise_z(1)
        for t in range(PACK):
            nc.vector.tensor_scalar(y_part[:, t, half:], y_banks[t][:, half:], 1.5, None, ALU.mult)
        h1 = [psum.tile([P, 2, half], F32, name="h1%d" % b, tag="h1%d" % b) for b in range(2)]
        for u in range(2):
            for b in range(2):
                second_product(1, 2 * u + b, h1[b][:, u, :])
            for b in range(2):
                take_size(1, 2 * u + b, 2 * u + b + 1, h1[b][:, u : u + 1, :])
            if u == 0:
                for b in range(2):
                    gain_h(1, b, h1[b][:, 0, :])
            for b in range(2):
                root_size(1, 2 * u + b, 2 * u + b + 1)
            for b in range(2):
                square_size(1, 2 * u + b)
        for b in range(2):
            gain_h_scalar(1, 2 + b, h1[b][:, 1, :])
        keep_y_scalar(2)
        keep_y_scalar(3)

        z2f = [sb("z2f%d" % c, [P, PACK, w], F32) for c, (c0, w) in enumerate(FIRST_CHUNKS)]
        for t, c in [(0, 0), (1, 0), (0, 1), (2, 0), (3, 0), (1, 1), (2, 1), (3, 1)]:
            c0, w = FIRST_CHUNKS[c]
            nc.vector.tensor_tensor(
                z2f[c][:, t, :], inv[t][:].indirect(n3_sb[:, c0 // 16 : (c0 + w) // 16]), h_gain[:, t, c0 : c0 + w], ALU.mult
            )

        ow = sb("ow", [P, S], U32)
        osc = sb("osc", [P, S], U8)
        out_rows = out_0.rearrange("(p t) s -> p t s", t=PACK)
        out_words = out_1[0].rearrange("p n t -> p (n t)").bitcast(I32)

        def weave(on_vector, dst, src):
            if on_vector:
                nc.vector.tensor_copy(out=woven(dst), in_=planar(src))
            else:
                nc.scalar.copy(out=woven(dst), in_=planar(src))

        def front(c):
            c0, w = LAST_CHUNKS[c]
            z2 = sb("z2_%d" % c, [P, PACK * w], BF16)
            weave(False, z2, z2f[c // 2][:, :, c0 % half : c0 % half + w])
            z2w = sb("z2w%d" % c, [P, w], U32)
            z2s = sb("z2s%d" % c, [P, w], U8)
            nc.vector.quantize_mx(out=z2w[:].bitcast(FP8X4), scales=z2s[:], in_=z2[:])
            bank = psum.tile([P, PACK, w], F32, name="o%d" % c, tag="h%d%d" % (c // 2, c % 2))
            for t in range(PACK):
                cols = slice(t * P, (t + 1) * P)
                nc.tensor.matmul_mx(
                    out=bank[:, t, :],
                    lhsT=w2w_d[:, cols].bitcast(FP8X4),
                    lhsT_scale=w2s_d[:, cols],
                    rhs=z2w[:].bitcast(FP8X4),
                    rhs_scale=z2s[:],
                    start=True,
                    stop=True,
                )
            return bank

        def middle(c, bank):
            c0, w = LAST_CHUNKS[c]
            res = sb("res%d" % c, [P, PACK, w], F32)
            nc.vector.tensor_tensor(res[:], bank[:], y_part[:, :, c0 : c0 + w], ALU.add)
            nc.sync.dma_start(out=out_rows[:, :, c0 : c0 + w], in_=res[:])
            rb = sb("rb%d" % c, [P, PACK * w], BF16)
            weave(c == 3, rb, res[:])
            return rb

        def back(c, rb):
            c0, w = LAST_CHUNKS[c]
            nc.vector.quantize_mx(out=ow[:, c0 : c0 + w].bitcast(FP8X4), scales=osc[:, c0 : c0 + w], in_=rb[:])
            nc.sync.dma_start(out=out_words[:, c0 : c0 + w], in_=ow[:, c0 : c0 + w].bitcast(I32))

        banks = [front(c) for c in range(4)]
        rounded = []
        for c in range(4):
            rounded.append(middle(c, banks[c]))
            if c > 0:
                back(c - 1, rounded[c - 1])
        back(3, rounded[3])
        scale_rows = out_2[0].bitcast(I32)
        for q in range(4):
            queue = nc.sync if q % 2 == 0 else nc.scalar
            queue.dma_start(out=scale_rows[4 * q : 4 * q + 4, :], in_=osc[32 * q : 32 * q + 4, :].bitcast(I32))
